import numpy as np, ml_dtypes
CORES = [44,45,46,47,172,173,174,175,300,301,302,303,428,429,430,431]
N = 16
GR, GC = 4, 4
L, KA, KB, F = 4, 1, 1, 512
def setup_inputs(rng):
    return {"a": rng.standard_normal((N, 128, KA * 128), dtype=np.float32).astype(ml_dtypes.bfloat16), "b": rng.standard_normal((N, 128, KB * F), dtype=np.float32).astype(ml_dtypes.bfloat16)}
def reference(a, b):
    A, B = a.astype(np.float64), b.astype(np.float64)
    y = np.zeros((N, 128, F))
    for i in range(GR):
        for j in range(GC):
            for k in range(L):
                At = A[i * GC + k // KA][:, 128 * (k % KA):128 * (k % KA) + 128]
                Bt = B[(k // KB) * GC + j][:, F * (k % KB):F * (k % KB) + F]
                y[i * GC + j] += At.T @ Bt
    return {"y": y.astype(ml_dtypes.bfloat16 if a.dtype != np.float64 else np.float64)}

@@ -1,0 +1,135 @@
+from concourse.bass import DstId, RemoteDMATransfer
+from concourse.mybir import AluOpType
+
+N, GR, GC, P, F = 16, 4, 4, 128, 512
+
+SCRATCH = {
+    "bsb": ("sbuf", [P, F], "bfloat16"),
+    "bland": ("sbuf", [P, F], "bfloat16"),
+    "asb": ("sbuf", [P, P], "bfloat16"),
+    "adram": ("dram", [P, P], "bfloat16"),
+    "aon": ("sbuf", [P, 2 * P], "bfloat16"),
+    "aland": ("dram", [2, P, P], "bfloat16"),
+    "afor": ("sbuf", [P, 2 * P], "bfloat16"),
+    "qsb": ("sbuf", [P, F], "bfloat16"),
+    "qland": ("sbuf", [P, F], "bfloat16"),
+    "ysb": ("sbuf", [P, F], "bfloat16"),
+    "pq": ("psum", [P, F], "float32"),
+    "py": ("psum", [P, F], "float32"),
+}
+SEMAPHORES = (["ld_b", "ld_ad", "ld_as", "al0", "al1", "barr", "qarr", "qdone", "ydone", "qready", "yready",
+               "stored", "sent"] + ["aa%d" % r for r in range(N)])
+
+
+def _bits(m):
+    return [e for e in range(m.bit_length()) if (m >> e) & 1]
+
+
+def _mk(es):
+    return sum(1 << e for e in es)
+
+
+def rank_program(g, core, T, topo):
+    rank = T.rank_of(core)
+    if rank is None:
+        return
+    cores, sem = T.cores, T.sem
+
+    def plan(r):
+        h, j = divmod(r, GC)
+        me = cores[r]
+        p = c = None
+        for o in range(GR):
+            oc = cores[o * GC + j]
+            if o == h or not topo.may_write(me, oc):
+                continue
+            if topo.rack(topo.host(oc)) == topo.rack(topo.host(me)):
+                p = o
+            else:
+                c = o
+        return (h, j, p, c) if j % 2 == 0 else (h, j, c, p)
+
+    def needs(r):
+        h, j, R, S = plan(r)
+        return [h * GC + h, h * GC + R, S * GC + h, S * GC + R]
+
+    def dst(r):
+        rid, pid = topo.addr(cores[r], core)
+        return DstId(rid=rid, pnc=pid)
+
+    def lanes(r):
+        hh, jj, RR, SS = plan(r)
+        out = _bits(topo.mask(cores[r], cores[RR * GC + jj]) & topo.mask(cores[r], cores[SS * GC + jj]))
+        return out, [e for e in _bits(topo.mask(cores[r], cores[hh * GC + (jj + 1) % GC])) if e not in out]
+
+    h, j, R, S = plan(rank)
+    mine = needs(rank)
+    takers = [(r2, s) for r2 in range(N) if r2 != rank for s, o in enumerate(needs(r2)) if o == rank]
+    near = [(r2, s) for r2, s in takers if s < 2]
+    far = [(r2, s) for r2, s in takers if s >= 2]
+    rawp, sump = cores[R * GC + j], cores[S * GC + j]
+    off, on = lanes(rank)
+    n_off, n_on = len(off), len(on)
+    sent = 0
+
+    g.sync.dma_start(T.bsb[:], T.b[:]).then_inc(sem.ld_b, 16)
+    if far:
+        g.scalar.dma_start(T.adram[:], T.a[:]).then_inc(sem.ld_ad, 16)
+    if near or rank in mine:
+        g.scalar.dma_start(T.asb[:], T.a[:]).then_inc(sem.ld_as, 16)
+
+    if far:
+        g.wait_ge(sem.ld_ad, 16)
+        g.remote_dma_fused([RemoteDMATransfer(
+            dst_ids=[dst(r2) for r2, s in far], dsts=[T.aland[s - 2] for r2, s in far], srcs=[T.adram[:]],
+            dma_engine_mask=_mk(off), remote_sem=sem["aa%d" % rank])], local_sem=sem.sent)
+        sent += n_off
+    g.wait_ge(sem.ld_b, 16)
+    rid, pid = topo.addr(rawp, core)
+    g.remote_dma(T.bland[:], T.bsb[:], sem.barr, sem.sent, pid, rid, _mk(off))
+    sent += n_off
+    if near:
+        g.wait_ge(sem.ld_as, 16)
+        g.remote_dma_fused([RemoteDMATransfer(
+            dst_ids=[dst(r2) for r2, s in near], dsts=[T.aon[:, s * P:(s + 1) * P] for r2, s in near],
+            srcs=[T.asb[:]], dma_engine_mask=_mk(on), remote_sem=sem["aa%d" % rank])], local_sem=sem.sent)
+        sent += n_on
+    g.wait_ge(sem.qready, 1)
+    rid, pid = topo.addr(sump, core)
+    g.remote_dma(T.qland[:], T.qsb[:], sem.qarr, sem.sent, pid, rid, _mk(off))
+    sent += n_off
+    g.wait_ge(sem.sent, sent)
+
+    g.scalar.wait_ge(sem["aa%d" % mine[2]], len(lanes(mine[2])[0]))
+    g.scalar.dma_start(T.afor[:, 0:P], T.aland[0]).then_inc(sem.al0, 16)
+    g.sync.wait_ge(sem["aa%d" % mine[3]], len(lanes(mine[3])[0]))
+    g.sync.dma_start(T.afor[:, P:2 * P], T.aland[1]).then_inc(sem.al1, 16)
+
+    t = g.tensor
+    t.wait_ge(sem.ld_b, 16)
+    t.wait_ge(sem.al0, 16)
+    t.matmul(T.pq[:], T.afor[:, 0:P], T.bsb[:], True, False)
+    t.wait_ge(sem.al1, 16)
+    t.wait_ge(sem.barr, n_off)
+    t.matmul(T.pq[:], T.afor[:, P:2 * P], T.bland[:], False, True).then_inc(sem.qdone, 1)
+    own = []
+    for s in (0, 1):
+        if mine[s] == rank:
+            t.wait_ge(sem.ld_as, 16)
+            own.append(T.asb[:])
+        else:
+            t.wait_ge(sem["aa%d" % mine[s]], len(lanes(mine[s])[1]))
+            own.append(T.aon[:, s * P:(s + 1) * P])
+    t.matmul(T.py[:], own[0], T.bsb[:], True, False)
+    t.matmul(T.py[:], own[1], T.bland[:], False, True).then_inc(sem.ydone, 1)
+
+    v = g.vector
+    v.wait_ge(sem.qdone, 1)
+    v.tensor_copy(T.qsb[:], T.pq[:]).then_inc(sem.qready, 1)
+    v.wait_ge(sem.ydone, 1)
+    v.wait_ge(sem.qarr, n_off)
+    v.tensor_tensor(T.ysb[:], T.py[:], T.qland[:], AluOpType.add).then_inc(sem.yready, 1)
+
+    g.sync.wait_ge(sem.yready, 1)
+    g.sync.dma_start(T.y[:], T.ysb[:]).then_inc(sem.stored, 16)
+    g.sync.wait_ge(sem.stored, 16)

@@ -1,24 +1,23 @@
 from concourse.bass import DstId, RemoteDMATransfer
-from concourse.mybir import AluOpType
 
 N, GR, GC, P, F = 16, 4, 4, 128, 512
+BLK = [(0, 192), (192, 384), (384, 512)]
+NB = len(BLK)
+VIA = 2
+ORDER = [0, 1, 2]
+PORT = True
 
 SCRATCH = {
     "bsb": ("sbuf", [P, F], "bfloat16"),
-    "bland": ("sbuf", [P, F], "bfloat16"),
-    "asb": ("sbuf", [P, P], "bfloat16"),
-    "adram": ("dram", [P, P], "bfloat16"),
-    "aon": ("sbuf", [P, 2 * P], "bfloat16"),
-    "aland": ("dram", [2, P, P], "bfloat16"),
-    "afor": ("sbuf", [P, 2 * P], "bfloat16"),
-    "qsb": ("sbuf", [P, F], "bfloat16"),
-    "qland": ("sbuf", [P, F], "bfloat16"),
+    "bl": ("sbuf", [P, 3 * F], "bfloat16"),
+    "hbuf": ("sbuf", [P, 128], "bfloat16"),
+    "hfull": ("sbuf", [P, F], "bfloat16"),
+    "arow": ("sbuf", [P, GC * P], "bfloat16"),
     "ysb": ("sbuf", [P, F], "bfloat16"),
-    "pq": ("psum", [P, F], "float32"),
-    "py": ("psum", [P, F], "float32"),
+    "py0": ("psum", [P, F], "float32"), "py1": ("psum", [P, F], "float32"), "py2": ("psum", [P, F], "float32"),
 }
-SEMAPHORES = (["ld_b", "ld_ad", "ld_as", "al0", "al1", "barr", "qarr", "qdone", "ydone", "qready", "yready",
-               "stored", "sent"] + ["aa%d" % r for r in range(N)])
+SEMAPHORES = (["ld_b", "ld_a", "arr1", "harr", "hfarr", "sent"] + ["aa%d" % k for k in range(GC)]
+              + [s % n for n in range(NB) for s in ("ca%d", "da%d", "yd%d", "yr%d", "st%d")])
 
 
 def _bits(m):
@@ -30,106 +29,134 @@ def _mk(es):
 
 
 def rank_program(g, core, T, topo):
-    rank = T.rank_of(core)
-    if rank is None:
-        return
     cores, sem = T.cores, T.sem
 
-    def plan(r):
-        h, j = divmod(r, GC)
-        me = cores[r]
-        p = c = None
+    def ring(r):
+        row, col = divmod(r, GC)
+        p = c = d = None
         for o in range(GR):
-            oc = cores[o * GC + j]
-            if o == h or not topo.may_write(me, oc):
+            oc = cores[o * GC + col]
+            if o == row:
                 continue
-            if topo.rack(topo.host(oc)) == topo.rack(topo.host(me)):
+            if not topo.may_write(cores[r], oc):
+                d = o
+            elif topo.rack(topo.host(oc)) == topo.rack(topo.host(cores[r])):
                 p = o
             else:
                 c = o
-        return (h, j, p, c) if j % 2 == 0 else (h, j, c, p)
+        return p, c, d
 
-    def needs(r):
-        h, j, R, S = plan(r)
-        return [h * GC + h, h * GC + R, S * GC + h, S * GC + R]
+    def carrier(r):
+        rc = cores[r]
+        span = topo.CORES_PER_CHIP
+        others = [x for x in range(max(0, rc - span), rc + span)
+                  if topo.host(x) == topo.host(rc) and topo.chip(x) == topo.chip(rc) and topo.die(x) != topo.die(rc)]
+        return others[r % GC]
 
-    def dst(r):
-        rid, pid = topo.addr(cores[r], core)
-        return DstId(rid=rid, pnc=pid)
+    def blk(ap_of, base, n):
+        return ap_of[:, base + BLK[n][0]:base + BLK[n][1]]
 
-    def lanes(r):
-        hh, jj, RR, SS = plan(r)
-        out = _bits(topo.mask(cores[r], cores[RR * GC + jj]) & topo.mask(cores[r], cores[SS * GC + jj]))
-        return out, [e for e in _bits(topo.mask(cores[r], cores[hh * GC + (jj + 1) % GC])) if e not in out]
+    rank = T.rank_of(core)
+    if rank is None:
+        if VIA is None and not PORT:
+            return
+        for r in range(N):
+            if carrier(r) == core:
+                total = 0
+                jobs = []
+                if VIA is not None:
+                    jobs.append((sem.harr, ring(r)[1], blk(T.bl, 0, VIA), T.hbuf[:], sem["ca%d" % VIA]))
+                if PORT:
+                    jobs.append((sem.hfarr, ring(r)[0], T.bl[:, F:2 * F], T.hfull[:], sem.arr1))
+                for wsem, row, out_ap, in_ap, rsem in jobs:
+                    target = cores[row * GC + r % GC]
+                    eng = _bits(topo.mask(core, target))
+                    rid, pid = topo.addr(target, core)
+                    g.wait_ge(wsem, len(_bits(topo.mask(cores[r], core))) - len(eng))
+                    g.remote_dma(out_ap, in_ap, rsem, sem.sent, pid, rid, _mk(eng))
+                    total += len(eng)
+                g.wait_ge(sem.sent, total)
+        return
 
-    h, j, R, S = plan(rank)
-    mine = needs(rank)
-    takers = [(r2, s) for r2 in range(N) if r2 != rank for s, o in enumerate(needs(r2)) if o == rank]
-    near = [(r2, s) for r2, s in takers if s < 2]
-    far = [(r2, s) for r2, s in takers if s >= 2]
-    rawp, sump = cores[R * GC + j], cores[S * GC + j]
-    off, on = lanes(rank)
+    h, j = divmod(rank, GC)
+    p, c, d = ring(rank)
+    at_p, at_c, help_me = cores[p * GC + j], cores[c * GC + j], carrier(rank)
+    off = _bits(topo.mask(core, at_p) & topo.mask(core, at_c))
+    on = [e for e in _bits(topo.mask(core, help_me)) if e not in off]
     n_off, n_on = len(off), len(on)
-    sent = 0
+    sent = [0]
+
+    def send(dst_core, out_ap, in_ap, rsem, engines):
+        rid, pid = topo.addr(dst_core, core)
+        g.remote_dma(out_ap, in_ap, rsem, sem.sent, pid, rid, _mk(engines))
+        sent[0] += len(engines)
+
+    def atile(k):
+        return T.arow[:, k * P:(k + 1) * P]
 
     g.sync.dma_start(T.bsb[:], T.b[:]).then_inc(sem.ld_b, 16)
-    if far:
-        g.scalar.dma_start(T.adram[:], T.a[:]).then_inc(sem.ld_ad, 16)
-    if near or rank in mine:
-        g.scalar.dma_start(T.asb[:], T.a[:]).then_inc(sem.ld_as, 16)
+    g.scalar.dma_start(atile(j), T.a[:]).then_inc(sem.ld_a, 16)
 
-    if far:
-        g.wait_ge(sem.ld_ad, 16)
-        g.remote_dma_fused([RemoteDMATransfer(
-            dst_ids=[dst(r2) for r2, s in far], dsts=[T.aland[s - 2] for r2, s in far], srcs=[T.adram[:]],
-            dma_engine_mask=_mk(off), remote_sem=sem["aa%d" % rank])], local_sem=sem.sent)
-        sent += n_off
     g.wait_ge(sem.ld_b, 16)
-    rid, pid = topo.addr(rawp, core)
-    g.remote_dma(T.bland[:], T.bsb[:], sem.barr, sem.sent, pid, rid, _mk(off))
-    sent += n_off
-    if near:
-        g.wait_ge(sem.ld_as, 16)
-        g.remote_dma_fused([RemoteDMATransfer(
-            dst_ids=[dst(r2) for r2, s in near], dsts=[T.aon[:, s * P:(s + 1) * P] for r2, s in near],
-            srcs=[T.asb[:]], dma_engine_mask=_mk(on), remote_sem=sem["aa%d" % rank])], local_sem=sem.sent)
-        sent += n_on
-    g.wait_ge(sem.qready, 1)
-    rid, pid = topo.addr(sump, core)
-    g.remote_dma(T.qland[:], T.qsb[:], sem.qarr, sem.sent, pid, rid, _mk(off))
-    sent += n_off
-    g.wait_ge(sem.sent, sent)
+    if VIA is not None:
+        send(help_me, T.hbuf[:], blk(T.bsb, 0, VIA), sem.harr, on)
+    for n in range(NB):
+        if n != VIA:
+            send(at_c, blk(T.bl, 0, n), blk(T.bsb, 0, n), sem["ca%d" % n], off)
+    if PORT:
+        send(help_me, T.hfull[:], T.bsb[:], sem.hfarr, on)
+    else:
+        send(at_p, T.bl[:, F:2 * F], T.bsb[:], sem.arr1, off)
+    g.wait_ge(sem.ld_a, 16)
+    ids = []
+    for k in range(GC):
+        if k != j:
+            rid, pid = topo.addr(cores[h * GC + k], core)
+            ids.append(DstId(rid=rid, pnc=pid))
+    g.remote_dma_fused([RemoteDMATransfer(dst_ids=ids, dsts=[atile(j) for q in ids], srcs=[atile(j)],
+                                          dma_engine_mask=_mk(on), remote_sem=sem["aa%d" % j])], local_sem=sem.sent)
+    sent[0] += n_on
+    for n in ORDER:
+        g.wait_ge(sem["ca%d" % n], n_off)
+        send(at_p, blk(T.bl, 2 * F, n), blk(T.bl, 0, n), sem["da%d" % n], off)
+    g.wait_ge(sem.sent, sent[0])
 
-    g.scalar.wait_ge(sem["aa%d" % mine[2]], len(lanes(mine[2])[0]))
-    g.scalar.dma_start(T.afor[:, 0:P], T.aland[0]).then_inc(sem.al0, 16)
-    g.sync.wait_ge(sem["aa%d" % mine[3]], len(lanes(mine[3])[0]))
-    g.sync.dma_start(T.afor[:, P:2 * P], T.aland[1]).then_inc(sem.al1, 16)
+    t, v = g.tensor, g.vector
+    py = [T.py0, T.py1, T.py2]
 
-    t = g.tensor
-    t.wait_ge(sem.ld_b, 16)
-    t.wait_ge(sem.al0, 16)
-    t.matmul(T.pq[:], T.afor[:, 0:P], T.bsb[:], True, False)
-    t.wait_ge(sem.al1, 16)
-    t.wait_ge(sem.barr, n_off)
-    t.matmul(T.pq[:], T.afor[:, P:2 * P], T.bland[:], False, True).then_inc(sem.qdone, 1)
-    own = []
-    for s in (0, 1):
-        if mine[s] == rank:
-            t.wait_ge(sem.ld_as, 16)
-            own.append(T.asb[:])
+    def term(k, buf, base, n, first, last):
+        w = BLK[n][1] - BLK[n][0]
+        return t.matmul(py[n][:, 0:w], atile(k), blk(buf, base, n), first, last)
+
+    def wait_a(k):
+        if k == j:
+            t.wait_ge(sem.ld_a, 16)
         else:
-            t.wait_ge(sem["aa%d" % mine[s]], len(lanes(mine[s])[1]))
-            own.append(T.aon[:, s * P:(s + 1) * P])
-    t.matmul(T.py[:], own[0], T.bsb[:], True, False)
-    t.matmul(T.py[:], own[1], T.bland[:], False, True).then_inc(sem.ydone, 1)
+            t.wait_ge(sem["aa%d" % k], n_on)
 
-    v = g.vector
-    v.wait_ge(sem.qdone, 1)
-    v.tensor_copy(T.qsb[:], T.pq[:]).then_inc(sem.qready, 1)
-    v.wait_ge(sem.ydone, 1)
-    v.wait_ge(sem.qarr, n_off)
-    v.tensor_tensor(T.ysb[:], T.py[:], T.qland[:], AluOpType.add).then_inc(sem.yready, 1)
+    t.wait_ge(sem.ld_b, 16)
+    wait_a(h)
+    for n in range(NB):
+        term(h, T.bsb, 0, n, True, False)
+    wait_a(p)
+    t.wait_ge(sem.arr1, n_off)
+    for n in range(NB):
+        term(p, T.bl, F, n, False, False)
+    wait_a(c)
+    for n in ORDER:
+        t.wait_ge(sem["ca%d" % n], n_off)
+        term(c, T.bl, 0, n, False, False)
+    wait_a(d)
+    for n in ORDER:
+        t.wait_ge(sem["da%d" % n], n_off)
+        term(d, T.bl, 2 * F, n, False, True).then_inc(sem["yd%d" % n], 1)
 
-    g.sync.wait_ge(sem.yready, 1)
-    g.sync.dma_start(T.y[:], T.ysb[:]).then_inc(sem.stored, 16)
-    g.sync.wait_ge(sem.stored, 16)
+    for n in ORDER:
+        v.wait_ge(sem["yd%d" % n], 1)
+        v.tensor_copy(blk(T.ysb, 0, n), py[n][:, 0:BLK[n][1] - BLK[n][0]]).then_inc(sem["yr%d" % n], 1)
+    queues = [g.sync, g.scalar, g.sync]
+    for q, n in zip(queues, ORDER):
+        q.wait_ge(sem["yr%d" % n], 1)
+        q.dma_start(blk(T.y, 0, n), blk(T.ysb, 0, n)).then_inc(sem["st%d" % n], 16)
+    for q, n in zip(queues, ORDER):
+        q.wait_ge(sem["st%d" % n], 16)

@@ -1,7 +1,7 @@
 from concourse.bass import DstId, RemoteDMATransfer
 
 N, GR, GC, P, F = 16, 4, 4, 128, 512
-BLK = [(0, 192), (192, 384), (384, 512)]
+BLK = [(0, 160), (160, 320), (320, 512)]
 NB = len(BLK)
 VIA = 2
 ORDER = [0, 1, 2]
@@ -10,7 +10,7 @@ PORT = True
 SCRATCH = {
     "bsb": ("sbuf", [P, F], "bfloat16"),
     "bl": ("sbuf", [P, 3 * F], "bfloat16"),
-    "hbuf": ("sbuf", [P, 128], "bfloat16"),
+    "hbuf": ("sbuf", [P, 192], "bfloat16"),
     "hfull": ("sbuf", [P, F], "bfloat16"),
     "arow": ("sbuf", [P, GC * P], "bfloat16"),
     "ysb": ("sbuf", [P, F], "bfloat16"),

from concourse.bass import DstId, RemoteDMATransfer

N, GR, GC, P, F = 16, 4, 4, 128, 512
BLK = [(0, 160), (160, 320), (320, 512)]
NB = len(BLK)
VIA = 2
ORDER = [0, 1, 2]
PORT = True

SCRATCH = {
    "bsb": ("sbuf", [P, F], "bfloat16"),
    "bl": ("sbuf", [P, 3 * F], "bfloat16"),
    "hbuf": ("sbuf", [P, 192], "bfloat16"),
    "hfull": ("sbuf", [P, F], "bfloat16"),
    "arow": ("sbuf", [P, GC * P], "bfloat16"),
    "ysb": ("sbuf", [P, F], "bfloat16"),
    "py0": ("psum", [P, F], "float32"), "py1": ("psum", [P, F], "float32"), "py2": ("psum", [P, F], "float32"),
}
SEMAPHORES = (["ld_b", "ld_a", "arr1", "harr", "hfarr", "sent"] + ["aa%d" % k for k in range(GC)]
              + [s % n for n in range(NB) for s in ("ca%d", "da%d", "yd%d", "yr%d", "st%d")])


def _bits(m):
    return [e for e in range(m.bit_length()) if (m >> e) & 1]


def _mk(es):
    return sum(1 << e for e in es)


def rank_program(g, core, T, topo):
    cores, sem = T.cores, T.sem

    def ring(r):
        row, col = divmod(r, GC)
        p = c = d = None
        for o in range(GR):
            oc = cores[o * GC + col]
            if o == row:
                continue
            if not topo.may_write(cores[r], oc):
                d = o
            elif topo.rack(topo.host(oc)) == topo.rack(topo.host(cores[r])):
                p = o
            else:
                c = o
        return p, c, d

    def carrier(r):
        rc = cores[r]
        span = topo.CORES_PER_CHIP
        others = [x for x in range(max(0, rc - span), rc + span)
                  if topo.host(x) == topo.host(rc) and topo.chip(x) == topo.chip(rc) and topo.die(x) != topo.die(rc)]
        return others[r % GC]

    def blk(ap_of, base, n):
        return ap_of[:, base + BLK[n][0]:base + BLK[n][1]]

    rank = T.rank_of(core)
    if rank is None:
        if VIA is None and not PORT:
            return
        for r in range(N):
            if carrier(r) == core:
                total = 0
                jobs = []
                if VIA is not None:
                    jobs.append((sem.harr, ring(r)[1], blk(T.bl, 0, VIA), T.hbuf[:], sem["ca%d" % VIA]))
                if PORT:
                    jobs.append((sem.hfarr, ring(r)[0], T.bl[:, F:2 * F], T.hfull[:], sem.arr1))
                for wsem, row, out_ap, in_ap, rsem in jobs:
                    target = cores[row * GC + r % GC]
                    eng = _bits(topo.mask(core, target))
                    rid, pid = topo.addr(target, core)
                    g.wait_ge(wsem, len(_bits(topo.mask(cores[r], core))) - len(eng))
                    g.remote_dma(out_ap, in_ap, rsem, sem.sent, pid, rid, _mk(eng))
                    total += len(eng)
                g.wait_ge(sem.sent, total)
        return

    h, j = divmod(rank, GC)
    p, c, d = ring(rank)
    at_p, at_c, help_me = cores[p * GC + j], cores[c * GC + j], carrier(rank)
    off = _bits(topo.mask(core, at_p) & topo.mask(core, at_c))
    on = [e for e in _bits(topo.mask(core, help_me)) if e not in off]
    n_off, n_on = len(off), len(on)
    sent = [0]

    def send(dst_core, out_ap, in_ap, rsem, engines):
        rid, pid = topo.addr(dst_core, core)
        g.remote_dma(out_ap, in_ap, rsem, sem.sent, pid, rid, _mk(engines))
        sent[0] += len(engines)

    def atile(k):
        return T.arow[:, k * P:(k + 1) * P]

    g.sync.dma_start(T.bsb[:], T.b[:]).then_inc(sem.ld_b, 16)
    g.scalar.dma_start(atile(j), T.a[:]).then_inc(sem.ld_a, 16)

    g.wait_ge(sem.ld_b, 16)
    if VIA is not None:
        send(help_me, T.hbuf[:], blk(T.bsb, 0, VIA), sem.harr, on)
    for n in range(NB):
        if n != VIA:
            send(at_c, blk(T.bl, 0, n), blk(T.bsb, 0, n), sem["ca%d" % n], off)
    if PORT:
        send(help_me, T.hfull[:], T.bsb[:], sem.hfarr, on)
    else:
        send(at_p, T.bl[:, F:2 * F], T.bsb[:], sem.arr1, off)
    g.wait_ge(sem.ld_a, 16)
    ids = []
    for k in range(GC):
        if k != j:
            rid, pid = topo.addr(cores[h * GC + k], core)
            ids.append(DstId(rid=rid, pnc=pid))
    g.remote_dma_fused([RemoteDMATransfer(dst_ids=ids, dsts=[atile(j) for q in ids], srcs=[atile(j)],
                                          dma_engine_mask=_mk(on), remote_sem=sem["aa%d" % j])], local_sem=sem.sent)
    sent[0] += n_on
    for n in ORDER:
        g.wait_ge(sem["ca%d" % n], n_off)
        send(at_p, blk(T.bl, 2 * F, n), blk(T.bl, 0, n), sem["da%d" % n], off)
    g.wait_ge(sem.sent, sent[0])

    t, v = g.tensor, g.vector
    py = [T.py0, T.py1, T.py2]

    def term(k, buf, base, n, first, last):
        w = BLK[n][1] - BLK[n][0]
        return t.matmul(py[n][:, 0:w], atile(k), blk(buf, base, n), first, last)

    def wait_a(k):
        if k == j:
            t.wait_ge(sem.ld_a, 16)
        else:
            t.wait_ge(sem["aa%d" % k], n_on)

    t.wait_ge(sem.ld_b, 16)
    wait_a(h)
    for n in range(NB):
        term(h, T.bsb, 0, n, True, False)
    wait_a(p)
    t.wait_ge(sem.arr1, n_off)
    for n in range(NB):
        term(p, T.bl, F, n, False, False)
    wait_a(c)
    for n in ORDER:
        t.wait_ge(sem["ca%d" % n], n_off)
        term(c, T.bl, 0, n, False, False)
    wait_a(d)
    for n in ORDER:
        t.wait_ge(sem["da%d" % n], n_off)
        term(d, T.bl, 2 * F, n, False, True).then_inc(sem["yd%d" % n], 1)

    for n in ORDER:
        v.wait_ge(sem["yd%d" % n], 1)
        v.tensor_copy(blk(T.ysb, 0, n), py[n][:, 0:BLK[n][1] - BLK[n][0]]).then_inc(sem["yr%d" % n], 1)
    queues = [g.sync, g.scalar, g.sync]
    for q, n in zip(queues, ORDER):
        q.wait_ge(sem["yr%d" % n], 1)
        q.dma_start(blk(T.y, 0, n), blk(T.ysb, 0, n)).then_inc(sem["st%d" % n], 16)
    for q, n in zip(queues, ORDER):
        q.wait_ge(sem["st%d" % n], 16)
